import numpy as np
import ml_dtypes


def mxq(x, axis, fmt="e4m3"):
    dtype, down = {"e4m3": (ml_dtypes.float8_e4m3fn, 7), "e5m2": (ml_dtypes.float8_e5m2, 14)}[fmt]
    v = np.moveaxis(np.asarray(x, np.float32).astype(ml_dtypes.bfloat16).astype(np.float64), axis, -1)
    blocks = v.reshape(v.shape[:-1] + (-1, 32))
    amax = np.abs(blocks).max(-1, keepdims=True)
    byte = np.maximum(np.where(amax > 0, np.frexp(amax)[1] - 1 + 127, 0) - down, 1)
    scale = np.exp2(byte - 127.0)
    codes = (blocks / scale).astype(np.float32).astype(dtype).astype(np.float64)
    return np.moveaxis((codes * scale).reshape(v.shape), -1, axis)


WIDE = False


def mx_kscale(k):
    if not WIDE:
        return np.ones(k)
    levels = np.array([10, -10, 5, -5, 0])
    if k % 512:
        return np.exp2(np.random.permutation(np.resize(levels, k // 32))).repeat(32)
    a = np.empty((k // 512, 16))
    for p in range(k // 512):
        a[p, :8] = np.random.permutation(np.resize(levels, 8))
        for g in range(8):
            far = levels[np.abs(levels - a[p, g]) >= 10]
            a[p, g + 8] = far[np.random.randint(len(far))]
    return np.exp2(a.ravel()).repeat(32)


def f64(x):
    return np.asarray(x).astype(np.float64)


def striped(idx):
    return np.tile(idx.reshape(-1, 16).T, (8, 1)).astype(np.uint16)


def unstriped(offs):
    return offs[:16].T.reshape(-1).astype(np.int64)


E2M1 = np.array([0.0, 0.5, 1.0, 1.5, 2.0, 3.0, 4.0, 6.0, -0.0, -0.5, -1.0, -1.5, -2.0, -3.0, -4.0, -6.0])


def pack_weight(w, fmt):
    k, n = w.shape
    w = f64(np.asarray(w, np.float32).astype(ml_dtypes.bfloat16)).reshape(k // 32, 32, n)
    amax = np.abs(w).max(1)
    if fmt == "e4m3":
        byte = np.frexp(amax)[1] - 1 + 127 - 7
    else:
        mant, ex = np.frexp(amax / 6.0)
        byte = np.where(mant > 0.5, ex, ex - 1) + 127
    byte = np.clip(np.where(amax > 0, byte, 1), 1, 254)
    scaled = (w * np.exp2(127.0 - byte)[:, None, :]).reshape(k, n).astype(np.float32)
    by_word = np.ascontiguousarray(scaled.reshape(k // 512, 128, 4, n).transpose(0, 1, 3, 2))
    if fmt == "e4m3":
        words = by_word.astype(ml_dtypes.float8_e4m3fn).view(np.uint8)
    else:
        c = by_word.astype(ml_dtypes.float4_e2m1fn).view(np.uint8) & 0xF
        words = (c[..., 0::2] | (c[..., 1::2] << 4)).reshape(k // 512, 128, 2 * n)
    return np.ascontiguousarray(words), np.ascontiguousarray(byte.astype(np.uint8).reshape(k // 512, 16, n))


def unpack_weight(words, scales, fmt):
    g, _, n = scales.shape
    words = np.ascontiguousarray(words).reshape(g, 128, n, -1)
    if fmt == "e4m3":
        vals = words.view(ml_dtypes.float8_e4m3fn).astype(np.float64)
    else:
        nib = np.empty((g, 128, n, 4), np.uint8)
        nib[..., 0::2] = words & 0xF
        nib[..., 1::2] = words >> 4
        vals = E2M1[nib]
    vals = vals * np.repeat(np.exp2(scales.astype(np.float64) - 127.0), 8, axis=1)[..., None]
    return vals.transpose(0, 1, 3, 2).reshape(g * 512, n)


def gelu(v):
    return 0.5 * v * (1.0 + np.tanh(np.sqrt(2.0 / np.pi) * (v + 0.044715 * v**3)))


K, M, T, S = 1536, 1024, 4096, 1536


def setup_inputs():
    n = np.random.standard_normal
    s = mx_kscale(K)[:, None]
    v = pack_weight(n((K, T)) * s, "e4m3")
    return {
        "tab_words": v[0],
        "tab_scales": v[1],
        "w": (n((K, M)) / np.sqrt(K) / s).astype(np.float32),
        "gT": n((M, T)).astype(np.float32),
        "b": (0.3 * n(1024)).astype(np.float32),
        "offs": striped(np.random.permutation(T)[:S]),
    }


def reference(tab_words, tab_scales, w, gT, b, offs):
    tab_ = unpack_weight(tab_words, tab_scales, "e4m3")[:, unstriped(offs)]
    w_ = mxq(f64(w), 0, "e4m3")
    y = w_.T @ tab_
    return (gelu(y + f64(b)[:, None])) * f64(gT)[:, unstriped(offs)]

@@ -1,0 +1,121 @@
+from contextlib import ExitStack
+
+import concourse.mybir as mybir
+from concourse.masks import make_identity
+
+K, M, T, S = 1536, 1024, 4096, 1536
+FLOPS = 2 * K * M * S
+
+F32 = mybir.dt.float32
+BF16 = mybir.dt.bfloat16
+I32 = mybir.dt.int32
+U32 = mybir.dt.uint32
+U16 = mybir.dt.uint16
+U8 = mybir.dt.uint8
+FP8X4 = mybir.dt.float8_e4m3fn_x4
+GELU = mybir.ActivationFunctionType.Gelu_apprx_tanh
+MULT = mybir.AluOpType.mult
+
+P = 128
+PACK = 4
+K_PASS = P * PACK
+PASSES = K // K_PASS
+N_TILE = 512
+M_TILES = M // P
+QUANT_COLS = 512
+STREAM_BUFS = 7
+
+
+def tile_list_tabgate_gelu_kernel(tc, tab_words, tab_scales, w, gT, b, offs, out):
+    nc = tc.nc
+    with ExitStack() as ctx:
+        keep = ctx.enter_context(tc.tile_pool(name="keep", bufs=1))
+        stream = ctx.enter_context(tc.tile_pool(name="stream", bufs=STREAM_BUFS))
+        stage = ctx.enter_context(tc.tile_pool(name="stage", bufs=2))
+        acts = ctx.enter_context(tc.tile_pool(name="acts", bufs=3))
+        results = ctx.enter_context(tc.tile_pool(name="results", bufs=M_TILES))
+        psum = ctx.enter_context(tc.psum_pool(name="psum", bufs=8))
+
+        offsets = keep.tile([P, S // 16], U16, name="offsets")
+        scale_table = keep.tile([P, T // 4], I32, name="scale_table", align_bytes=64)
+        bias_rows = keep.tile([P, P], F32, name="bias_rows")
+        identity = keep.tile([P, P], F32, name="identity")
+        bias = keep.tile([P, M_TILES], F32, name="bias")
+        w_codes = keep.tile([P, PASSES, M], U32, name="w_codes", align_bytes=64)
+        w_scales = keep.tile([P, PASSES, M], U8, name="w_scales", align_bytes=64)
+        v_scales = keep.tile([P, S], U8, name="v_scales", align_bytes=64)
+        v_codes = [keep.tile([P, S], U32, name=f"v_codes{a}", align_bytes=64) for a in range(PASSES)]
+
+        nc.vector.memset(scale_table[:], 0)
+        nc.vector.memset(bias_rows[:], 0.0)
+        scale_words = tab_scales.bitcast(I32)
+        for q in range(4):
+            nc.gpsimd.dma_start(
+                out=scale_table[32 * q : 32 * q + 4 * PASSES, :], in_=scale_words[:, 4 * q : 4 * q + 4, :]
+            )
+        nc.gpsimd.dma_start(out=bias_rows[0:M_TILES, :], in_=b.rearrange("(m p) -> m p", p=P))
+        make_identity(nc, identity[:])
+
+        w_raw = []
+        for a in range(PASSES):
+            raw = stream.tile([P, PACK, M], F32, name="stream")
+            nc.sync.dma_start(out=raw[:], in_=w[a * K_PASS : (a + 1) * K_PASS, :].rearrange("(p j) n -> p j n", j=PACK))
+            w_raw.append(raw)
+            if a == 0:
+                nc.sync.dma_start(offsets[:], offs)
+        tables = []
+        for a in range(PASSES):
+            table = stream.tile([P, T], I32, name="stream")
+            nc.sync.dma_start(out=table[:], in_=tab_words[a].rearrange("p t i -> p (t i)").bitcast(I32))
+            tables.append(table)
+
+        bias_bank = psum.tile([P, P], F32, name="bank")
+        nc.tensor.transpose(bias_bank[:], bias_rows[:], identity[:])
+        nc.vector.tensor_copy(out=bias[:], in_=bias_bank[:, 0:M_TILES])
+
+        for a in range(PASSES):
+            for n0 in range(0, M, QUANT_COLS):
+                cols = slice(n0, n0 + QUANT_COLS)
+                grouped = stage.tile([P, QUANT_COLS, PACK], BF16, name="grouped", align_bytes=64)
+                nc.scalar.copy(out=grouped[:], in_=w_raw[a][:, :, cols].rearrange("p j n -> p n j"))
+                nc.vector.quantize_mx(
+                    out=w_codes[:, a, cols].bitcast(FP8X4),
+                    scales=w_scales[:, a, cols],
+                    in_=grouped[:].rearrange("p n j -> p (n j)"),
+                )
+
+        gates = []
+        for m in range(M_TILES):
+            gate = stream.tile([P, T], F32, name="stream")
+            nc.sync.dma_start(out=gate[:], in_=gT[m * P : (m + 1) * P, :])
+            gates.append(gate)
+            if m == 0:
+                nc.vector.tensor_copy(v_scales[:], scale_table[:].bitcast(U8).indirect(offsets[:]))
+                for a in range(PASSES):
+                    nc.vector.tensor_copy(v_codes[a][:], tables[a][:].bitcast(U32).indirect(offsets[:]))
+            if m >= STREAM_BUFS - 1:
+                finish(nc, psum, acts, results, m - (STREAM_BUFS - 1), gates, offsets, w_codes, w_scales, v_codes, v_scales, bias, out)
+        for m in range(M_TILES - (STREAM_BUFS - 1), M_TILES):
+            finish(nc, psum, acts, results, m, gates, offsets, w_codes, w_scales, v_codes, v_scales, bias, out)
+
+
+def finish(nc, psum, acts, results, m, gates, offsets, w_codes, w_scales, v_codes, v_scales, bias, out):
+    rows = slice(m * P, (m + 1) * P)
+    act = acts.tile([P, S], F32, name="act")
+    for j0 in range(0, S, N_TILE):
+        cols = slice(j0, j0 + N_TILE)
+        bank = psum.tile([P, N_TILE], F32, name="bank")
+        for a in range(PASSES):
+            nc.tensor.matmul_mx(
+                out=bank[:],
+                lhsT=w_codes[:, a, rows].bitcast(FP8X4),
+                lhsT_scale=w_scales[:, a, rows],
+                rhs=v_codes[a][:, cols].bitcast(FP8X4),
+                rhs_scale=v_scales[4 * a : P, cols],
+                start=(a == 0),
+                stop=(a == PASSES - 1),
+            )
+        nc.scalar.activation(out=act[:, cols], in_=bank[:], func=GELU, bias=bias[:, m : m + 1])
+    result = results.tile([P, S], F32, name="result")
+    nc.vector.tensor_tensor(result[:], gates[m][:].indirect(offsets[:]), act[:], MULT)
+    nc.sync.dma_start(out=out[rows, :], in_=result[:])

@@ -1,7 +1,6 @@
 from contextlib import ExitStack
 
 import concourse.mybir as mybir
-from concourse.masks import make_identity
 
 K, M, T, S = 1536, 1024, 4096, 1536
 FLOPS = 2 * K * M * S
@@ -22,8 +21,9 @@ K_PASS = P * PACK
 PASSES = K // K_PASS
 N_TILE = 512
 M_TILES = M // P
-QUANT_COLS = 512
+QUANT_TILES = 4
 STREAM_BUFS = 7
+STORE_ENDS = (4, 7, 8)
 
 
 def tile_list_tabgate_gelu_kernel(tc, tab_words, tab_scales, w, gT, b, offs, out):
@@ -31,91 +31,85 @@ def tile_list_tabgate_gelu_kernel(tc, tab_words, tab_scales, w, gT, b, offs, out
     with ExitStack() as ctx:
         keep = ctx.enter_context(tc.tile_pool(name="keep", bufs=1))
         stream = ctx.enter_context(tc.tile_pool(name="stream", bufs=STREAM_BUFS))
-        stage = ctx.enter_context(tc.tile_pool(name="stage", bufs=2))
+        stage = ctx.enter_context(tc.tile_pool(name="stage", bufs=3))
         acts = ctx.enter_context(tc.tile_pool(name="acts", bufs=3))
-        results = ctx.enter_context(tc.tile_pool(name="results", bufs=M_TILES))
         psum = ctx.enter_context(tc.psum_pool(name="psum", bufs=8))
 
         offsets = keep.tile([P, S // 16], U16, name="offsets")
         scale_table = keep.tile([P, T // 4], I32, name="scale_table", align_bytes=64)
-        bias_rows = keep.tile([P, P], F32, name="bias_rows")
-        identity = keep.tile([P, P], F32, name="identity")
         bias = keep.tile([P, M_TILES], F32, name="bias")
         w_codes = keep.tile([P, PASSES, M], U32, name="w_codes", align_bytes=64)
         w_scales = keep.tile([P, PASSES, M], U8, name="w_scales", align_bytes=64)
         v_scales = keep.tile([P, S], U8, name="v_scales", align_bytes=64)
         v_codes = [keep.tile([P, S], U32, name=f"v_codes{a}", align_bytes=64) for a in range(PASSES)]
+        result = keep.tile([P, M_TILES, S], F32, name="result")
 
         nc.vector.memset(scale_table[:], 0)
-        nc.vector.memset(bias_rows[:], 0.0)
         scale_words = tab_scales.bitcast(I32)
         for q in range(4):
             nc.gpsimd.dma_start(
                 out=scale_table[32 * q : 32 * q + 4 * PASSES, :], in_=scale_words[:, 4 * q : 4 * q + 4, :]
             )
-        nc.gpsimd.dma_start(out=bias_rows[0:M_TILES, :], in_=b.rearrange("(m p) -> m p", p=P))
-        make_identity(nc, identity[:])
 
-        w_raw = []
-        for a in range(PASSES):
-            raw = stream.tile([P, PACK, M], F32, name="stream")
-            nc.sync.dma_start(out=raw[:], in_=w[a * K_PASS : (a + 1) * K_PASS, :].rearrange("(p j) n -> p j n", j=PACK))
-            w_raw.append(raw)
-            if a == 0:
-                nc.sync.dma_start(offsets[:], offs)
         tables = []
         for a in range(PASSES):
             table = stream.tile([P, T], I32, name="stream")
             nc.sync.dma_start(out=table[:], in_=tab_words[a].rearrange("p t i -> p (t i)").bitcast(I32))
             tables.append(table)
-
-        bias_bank = psum.tile([P, P], F32, name="bank")
-        nc.tensor.transpose(bias_bank[:], bias_rows[:], identity[:])
-        nc.vector.tensor_copy(out=bias[:], in_=bias_bank[:, 0:M_TILES])
-
+            if a == 0:
+                nc.sync.dma_start(offsets[:], offs)
+                nc.sync.dma_start(out=bias[:], in_=b.rearrange("(p m) -> p m", m=M_TILES))
+        w_raw = []
         for a in range(PASSES):
-            for n0 in range(0, M, QUANT_COLS):
-                cols = slice(n0, n0 + QUANT_COLS)
-                grouped = stage.tile([P, QUANT_COLS, PACK], BF16, name="grouped", align_bytes=64)
-                nc.scalar.copy(out=grouped[:], in_=w_raw[a][:, :, cols].rearrange("p j n -> p n j"))
-                nc.vector.quantize_mx(
-                    out=w_codes[:, a, cols].bitcast(FP8X4),
-                    scales=w_scales[:, a, cols],
-                    in_=grouped[:].rearrange("p n j -> p (n j)"),
-                )
-
+            raw = stream.tile([P, PACK, M], F32, name="stream")
+            nc.sync.dma_start(out=raw[:], in_=w[a * K_PASS : (a + 1) * K_PASS, :].rearrange("(p j) n -> p j n", j=PACK))
+            w_raw.append(raw)
         gates = []
         for m in range(M_TILES):
             gate = stream.tile([P, T], F32, name="stream")
-            nc.sync.dma_start(out=gate[:], in_=gT[m * P : (m + 1) * P, :])
+            nc.sync.dma_start(out=gate[:], in_=gT.rearrange("(p m) t -> m p t", m=M_TILES)[m])
             gates.append(gate)
-            if m == 0:
-                nc.vector.tensor_copy(v_scales[:], scale_table[:].bitcast(U8).indirect(offsets[:]))
-                for a in range(PASSES):
-                    nc.vector.tensor_copy(v_codes[a][:], tables[a][:].bitcast(U32).indirect(offsets[:]))
-            if m >= STREAM_BUFS - 1:
-                finish(nc, psum, acts, results, m - (STREAM_BUFS - 1), gates, offsets, w_codes, w_scales, v_codes, v_scales, bias, out)
-        for m in range(M_TILES - (STREAM_BUFS - 1), M_TILES):
-            finish(nc, psum, acts, results, m, gates, offsets, w_codes, w_scales, v_codes, v_scales, bias, out)
 
-
-def finish(nc, psum, acts, results, m, gates, offsets, w_codes, w_scales, v_codes, v_scales, bias, out):
-    rows = slice(m * P, (m + 1) * P)
-    act = acts.tile([P, S], F32, name="act")
-    for j0 in range(0, S, N_TILE):
-        cols = slice(j0, j0 + N_TILE)
-        bank = psum.tile([P, N_TILE], F32, name="bank")
         for a in range(PASSES):
-            nc.tensor.matmul_mx(
-                out=bank[:],
-                lhsT=w_codes[:, a, rows].bitcast(FP8X4),
-                lhsT_scale=w_scales[:, a, rows],
-                rhs=v_codes[a][:, cols].bitcast(FP8X4),
-                rhs_scale=v_scales[4 * a : P, cols],
-                start=(a == 0),
-                stop=(a == PASSES - 1),
-            )
-        nc.scalar.activation(out=act[:, cols], in_=bank[:], func=GELU, bias=bias[:, m : m + 1])
-    result = results.tile([P, S], F32, name="result")
-    nc.vector.tensor_tensor(result[:], gates[m][:].indirect(offsets[:]), act[:], MULT)
-    nc.sync.dma_start(out=out[rows, :], in_=result[:])
+            nc.vector.tensor_copy(v_codes[a][:], tables[a][:].bitcast(U32).indirect(offsets[:]))
+        nc.vector.tensor_copy(v_scales[:], scale_table[:].bitcast(U8).indirect(offsets[:]))
+
+        for a in range(PASSES):
+            for m0 in range(0, M_TILES, QUANT_TILES):
+                cols = slice(m0 * P, (m0 + QUANT_TILES) * P)
+                grouped = stage.tile([P, QUANT_TILES, P, PACK], BF16, name="grouped", align_bytes=64)
+                source = w_raw[a][:].rearrange("p j (q m) -> p q m j", m=M_TILES)[:, :, m0 : m0 + QUANT_TILES, :]
+                target = grouped[:].rearrange("p m q j -> p q m j")
+                if a == PASSES - 1 and m0 == 0:
+                    nc.vector.tensor_copy(out=target, in_=source)
+                else:
+                    nc.scalar.copy(out=target, in_=source)
+                nc.vector.quantize_mx(
+                    out=w_codes[:, a, cols].bitcast(FP8X4),
+                    scales=w_scales[:, a, cols],
+                    in_=grouped[:].rearrange("p m q j -> p (m q j)"),
+                )
+
+        out_rows = out.rearrange("(p m) j -> p m j", m=M_TILES)
+        stored = 0
+        for m in range(M_TILES):
+            rows = slice(m * P, (m + 1) * P)
+            act = acts.tile([P, S], F32, name="act")
+            for j0 in range(0, S, N_TILE):
+                cols = slice(j0, j0 + N_TILE)
+                bank = psum.tile([P, N_TILE], F32, name="bank")
+                for a in range(PASSES):
+                    nc.tensor.matmul_mx(
+                        out=bank[:],
+                        lhsT=w_codes[:, a, rows].bitcast(FP8X4),
+                        lhsT_scale=w_scales[:, a, rows],
+                        rhs=v_codes[a][:, cols].bitcast(FP8X4),
+                        rhs_scale=v_scales[4 * a : P, cols],
+                        start=(a == 0),
+                        stop=(a == PASSES - 1),
+                    )
+                nc.scalar.activation(out=act[:, cols], in_=bank[:], func=GELU, bias=bias[:, m : m + 1])
+            nc.vector.tensor_tensor(result[:, m, :], gates[m][:].indirect(offsets[:]), act[:], MULT)
+            if m + 1 in STORE_ENDS:
+                nc.sync.dma_start(out=out_rows[:, stored : m + 1, :], in_=result[:, stored : m + 1, :])
+                stored = m + 1

@@ -23,7 +23,7 @@ N_TILE = 512
 M_TILES = M // P
 QUANT_TILES = 4
 STREAM_BUFS = 7
-STORE_ENDS = (4, 7, 8)
+VECTOR_CASTS = ((1, 4), (2, 0))
 
 
 def tile_list_tabgate_gelu_kernel(tc, tab_words, tab_scales, w, gT, b, offs, out):
@@ -80,7 +80,7 @@ def tile_list_tabgate_gelu_kernel(tc, tab_words, tab_scales, w, gT, b, offs, out
                 grouped = stage.tile([P, QUANT_TILES, P, PACK], BF16, name="grouped", align_bytes=64)
                 source = w_raw[a][:].rearrange("p j (q m) -> p q m j", m=M_TILES)[:, :, m0 : m0 + QUANT_TILES, :]
                 target = grouped[:].rearrange("p m q j -> p q m j")
-                if a == PASSES - 1 and m0 == 0:
+                if (a, m0) in VECTOR_CASTS:
                     nc.vector.tensor_copy(out=target, in_=source)
                 else:
                     nc.scalar.copy(out=target, in_=source)
@@ -91,7 +91,6 @@ def tile_list_tabgate_gelu_kernel(tc, tab_words, tab_scales, w, gT, b, offs, out
                 )
 
         out_rows = out.rearrange("(p m) j -> p m j", m=M_TILES)
-        stored = 0
         for m in range(M_TILES):
             rows = slice(m * P, (m + 1) * P)
             act = acts.tile([P, S], F32, name="act")
@@ -109,7 +108,9 @@ def tile_list_tabgate_gelu_kernel(tc, tab_words, tab_scales, w, gT, b, offs, out
                         stop=(a == PASSES - 1),
                     )
                 nc.scalar.activation(out=act[:, cols], in_=bank[:], func=GELU, bias=bias[:, m : m + 1])
-            nc.vector.tensor_tensor(result[:, m, :], gates[m][:].indirect(offsets[:]), act[:], MULT)
-            if m + 1 in STORE_ENDS:
-                nc.sync.dma_start(out=out_rows[:, stored : m + 1, :], in_=result[:, stored : m + 1, :])
-                stored = m + 1
+            width = N_TILE if m == M_TILES - 1 else S
+            for j0 in range(0, S, width):
+                cols = slice(j0, j0 + width)
+                picks = offsets[:, j0 // 16 : (j0 + width) // 16]
+                nc.vector.tensor_tensor(result[:, m, cols], gates[m][:].indirect(picks), act[:, cols], MULT)
+                nc.sync.dma_start(out=out_rows[:, m, cols], in_=result[:, m, cols])

@@ -23,6 +23,8 @@ N_TILE = 512
 M_TILES = M // P
 QUANT_TILES = 4
 STREAM_BUFS = 7
+STORE_ENDS = (1, 2, 3, 6, 7, 8)
+EARLY_STORES = 3
 VECTOR_CASTS = ((1, 4), (2, 0))
 
 
@@ -91,6 +93,7 @@ def tile_list_tabgate_gelu_kernel(tc, tab_words, tab_scales, w, gT, b, offs, out
                 )
 
         out_rows = out.rearrange("(p m) j -> p m j", m=M_TILES)
+        stored = 0
         for m in range(M_TILES):
             rows = slice(m * P, (m + 1) * P)
             act = acts.tile([P, S], F32, name="act")
@@ -108,9 +111,8 @@ def tile_list_tabgate_gelu_kernel(tc, tab_words, tab_scales, w, gT, b, offs, out
                         stop=(a == PASSES - 1),
                     )
                 nc.scalar.activation(out=act[:, cols], in_=bank[:], func=GELU, bias=bias[:, m : m + 1])
-            width = N_TILE if m == M_TILES - 1 else S
-            for j0 in range(0, S, width):
-                cols = slice(j0, j0 + width)
-                picks = offsets[:, j0 // 16 : (j0 + width) // 16]
-                nc.vector.tensor_tensor(result[:, m, cols], gates[m][:].indirect(picks), act[:, cols], MULT)
-                nc.sync.dma_start(out=out_rows[:, m, cols], in_=result[:, m, cols])
+            nc.vector.tensor_tensor(result[:, m, :], gates[m][:].indirect(offsets[:]), act[:], MULT)
+            if m + 1 in STORE_ENDS:
+                queue = nc.scalar if m < EARLY_STORES else nc.sync
+                queue.dma_start(out=out_rows[:, stored : m + 1, :], in_=result[:, stored : m + 1, :])
+                stored = m + 1

@@ -42,16 +42,17 @@ def tile_list_tabgate_gelu_kernel(tc, tab_words, tab_scales, w, gT, b, offs, out
         bias = keep.tile([P, M_TILES], F32, name="bias")
         w_codes = keep.tile([P, PASSES, M], U32, name="w_codes", align_bytes=64)
         w_scales = keep.tile([P, PASSES, M], U8, name="w_scales", align_bytes=64)
-        v_scales = keep.tile([P, S], U8, name="v_scales", align_bytes=64)
+        picked_scales = keep.tile([P, S], U8, name="picked_scales", align_bytes=64)
+        v_scales = keep.tile([P, S // 4], I32, name="v_scales", align_bytes=64)
         v_codes = [keep.tile([P, S], U32, name=f"v_codes{a}", align_bytes=64) for a in range(PASSES)]
         result = keep.tile([P, M_TILES, S], F32, name="result")
 
         nc.vector.memset(scale_table[:], 0)
         scale_words = tab_scales.bitcast(I32)
-        for q in range(4):
-            nc.gpsimd.dma_start(
-                out=scale_table[32 * q : 32 * q + 4 * PASSES, :], in_=scale_words[:, 4 * q : 4 * q + 4, :]
-            )
+        nc.sync.dma_start(offsets[:], offs)
+        for a in range(PASSES):
+            nc.scalar.dma_start(out=scale_table[32 + a : 96 : 4, :], in_=scale_words[a])
+        nc.vector.memset(v_scales[:], 0)
 
         tables = []
         for a in range(PASSES):
@@ -59,7 +60,6 @@ def tile_list_tabgate_gelu_kernel(tc, tab_words, tab_scales, w, gT, b, offs, out
             nc.sync.dma_start(out=table[:], in_=tab_words[a].rearrange("p t i -> p (t i)").bitcast(I32))
             tables.append(table)
             if a == 0:
-                nc.sync.dma_start(offsets[:], offs)
                 nc.sync.dma_start(out=bias[:], in_=b.rearrange("(p m) -> p m", m=M_TILES))
         w_raw = []
         for a in range(PASSES):
@@ -72,9 +72,14 @@ def tile_list_tabgate_gelu_kernel(tc, tab_words, tab_scales, w, gT, b, offs, out
             nc.sync.dma_start(out=gate[:], in_=gT.rearrange("(p m) t -> m p t", m=M_TILES)[m])
             gates.append(gate)
 
+        nc.vector.tensor_copy(picked_scales[:], scale_table[:].bitcast(U8).indirect(offsets[:]))
+        for a in range(PASSES):
+            for r in range(4):
+                nc.gpsimd.dma_start(
+                    out=v_scales[4 * a + r : P : 32, :], in_=picked_scales[32 + 4 * r + a : 96 : 16, :].bitcast(I32)
+                )
         for a in range(PASSES):
             nc.vector.tensor_copy(v_codes[a][:], tables[a][:].bitcast(U32).indirect(offsets[:]))
-        nc.vector.tensor_copy(v_scales[:], scale_table[:].bitcast(U8).indirect(offsets[:]))
 
         for a in range(PASSES):
             for m0 in range(0, M_TILES, QUANT_TILES):
@@ -106,7 +111,7 @@ def tile_list_tabgate_gelu_kernel(tc, tab_words, tab_scales, w, gT, b, offs, out
                         lhsT=w_codes[:, a, rows].bitcast(FP8X4),
                         lhsT_scale=w_scales[:, a, rows],
                         rhs=v_codes[a][:, cols].bitcast(FP8X4),
-                        rhs_scale=v_scales[4 * a : P, cols],
+                        rhs_scale=v_scales[4 * a : P, :].bitcast(U8)[:, cols],
                         start=(a == 0),
                         stop=(a == PASSES - 1),
                     )

@@ -25,7 +25,6 @@ QUANT_TILES = 4
 STREAM_BUFS = 7
 STORE_ENDS = (1, 2, 3, 6, 7, 8)
 EARLY_STORES = 3
-VECTOR_CASTS = ((1, 4), (2, 0))
 
 
 def tile_list_tabgate_gelu_kernel(tc, tab_words, tab_scales, w, gT, b, offs, out):
@@ -51,21 +50,21 @@ def tile_list_tabgate_gelu_kernel(tc, tab_words, tab_scales, w, gT, b, offs, out
         scale_words = tab_scales.bitcast(I32)
         nc.sync.dma_start(offsets[:], offs)
         for a in range(PASSES):
-            nc.scalar.dma_start(out=scale_table[32 + a : 96 : 4, :], in_=scale_words[a])
+            nc.gpsimd.dma_start(out=scale_table[32 + a : 96 : 4, :], in_=scale_words[a])
         nc.vector.memset(v_scales[:], 0)
 
-        tables = []
-        for a in range(PASSES):
-            table = stream.tile([P, T], I32, name="stream")
-            nc.sync.dma_start(out=table[:], in_=tab_words[a].rearrange("p t i -> p (t i)").bitcast(I32))
-            tables.append(table)
-            if a == 0:
-                nc.sync.dma_start(out=bias[:], in_=b.rearrange("(p m) -> p m", m=M_TILES))
         w_raw = []
         for a in range(PASSES):
             raw = stream.tile([P, PACK, M], F32, name="stream")
             nc.sync.dma_start(out=raw[:], in_=w[a * K_PASS : (a + 1) * K_PASS, :].rearrange("(p j) n -> p j n", j=PACK))
             w_raw.append(raw)
+            if a == 0:
+                nc.sync.dma_start(out=bias[:], in_=b.rearrange("(p m) -> p m", m=M_TILES))
+        tables = []
+        for a in range(PASSES):
+            table = stream.tile([P, T], I32, name="stream")
+            nc.sync.dma_start(out=table[:], in_=tab_words[a].rearrange("p t i -> p (t i)").bitcast(I32))
+            tables.append(table)
         gates = []
         for m in range(M_TILES):
             gate = stream.tile([P, T], F32, name="stream")
@@ -78,8 +77,6 @@ def tile_list_tabgate_gelu_kernel(tc, tab_words, tab_scales, w, gT, b, offs, out
                 nc.gpsimd.dma_start(
                     out=v_scales[4 * a + r : P : 32, :], in_=picked_scales[32 + 4 * r + a : 96 : 16, :].bitcast(I32)
                 )
-        for a in range(PASSES):
-            nc.vector.tensor_copy(v_codes[a][:], tables[a][:].bitcast(U32).indirect(offsets[:]))
 
         for a in range(PASSES):
             for m0 in range(0, M_TILES, QUANT_TILES):
@@ -87,15 +84,18 @@ def tile_list_tabgate_gelu_kernel(tc, tab_words, tab_scales, w, gT, b, offs, out
                 grouped = stage.tile([P, QUANT_TILES, P, PACK], BF16, name="grouped", align_bytes=64)
                 source = w_raw[a][:].rearrange("p j (q m) -> p q m j", m=M_TILES)[:, :, m0 : m0 + QUANT_TILES, :]
                 target = grouped[:].rearrange("p m q j -> p q m j")
-                if (a, m0) in VECTOR_CASTS:
-                    nc.vector.tensor_copy(out=target, in_=source)
-                else:
-                    nc.scalar.copy(out=target, in_=source)
+                nc.scalar.copy(out=target, in_=source)
                 nc.vector.quantize_mx(
                     out=w_codes[:, a, cols].bitcast(FP8X4),
                     scales=w_scales[:, a, cols],
                     in_=grouped[:].rearrange("p m q j -> p (m q j)"),
                 )
+
+        for a in range(PASSES):
+            width = N_TILE if a == PASSES - 1 else S
+            for j0 in range(0, S, width):
+                picks = offsets[:, j0 // 16 : (j0 + width) // 16]
+                nc.vector.tensor_copy(v_codes[a][:, j0 : j0 + width], tables[a][:].bitcast(U32).indirect(picks))
 
         out_rows = out.rearrange("(p m) j -> p m j", m=M_TILES)
         stored = 0

@@ -72,10 +72,12 @@ def tile_list_tabgate_gelu_kernel(tc, tab_words, tab_scales, w, gT, b, offs, out
             gates.append(gate)
 
         nc.vector.tensor_copy(picked_scales[:], scale_table[:].bitcast(U8).indirect(offsets[:]))
-        for a in range(PASSES):
-            for r in range(4):
+        for r in range(4):
+            for q in (0, 2, 1, 3):
+                first = 32 + 4 * (4 * q + r)
                 nc.gpsimd.dma_start(
-                    out=v_scales[4 * a + r : P : 32, :], in_=picked_scales[32 + 4 * r + a : 96 : 16, :].bitcast(I32)
+                    out=v_scales[32 * q + r : 32 * q + 4 * PASSES : 4, :],
+                    in_=picked_scales[first : first + PASSES, :].bitcast(I32),
                 )
 
         for a in range(PASSES):

@@ -50,7 +50,8 @@ def tile_list_tabgate_gelu_kernel(tc, tab_words, tab_scales, w, gT, b, offs, out
         scale_words = tab_scales.bitcast(I32)
         nc.sync.dma_start(offsets[:], offs)
         for a in range(PASSES):
-            nc.gpsimd.dma_start(out=scale_table[32 + a : 96 : 4, :], in_=scale_words[a])
+            for i0 in (0, 8):
+                nc.gpsimd.dma_start(out=scale_table[4 * i0 + a : 4 * i0 + 32 : 4, :], in_=scale_words[a, i0 : i0 + 8])
         nc.vector.memset(v_scales[:], 0)
 
         w_raw = []
@@ -74,7 +75,7 @@ def tile_list_tabgate_gelu_kernel(tc, tab_words, tab_scales, w, gT, b, offs, out
         nc.vector.tensor_copy(picked_scales[:], scale_table[:].bitcast(U8).indirect(offsets[:]))
         for r in range(4):
             for q in (0, 2, 1, 3):
-                first = 32 + 4 * (4 * q + r)
+                first = 4 * (4 * q + r)
                 nc.gpsimd.dma_start(
                     out=v_scales[32 * q + r : 32 * q + 4 * PASSES : 4, :],
                     in_=picked_scales[first : first + PASSES, :].bitcast(I32),

@@ -23,7 +23,7 @@ N_TILE = 512
 M_TILES = M // P
 QUANT_TILES = 4
 STREAM_BUFS = 7
-STORE_ENDS = (1, 2, 3, 6, 7, 8)
+STORE_ENDS = (1, 2, 3, 6, 7)
 EARLY_STORES = 3
 
 
@@ -119,7 +119,14 @@ def tile_list_tabgate_gelu_kernel(tc, tab_words, tab_scales, w, gT, b, offs, out
                         stop=(a == PASSES - 1),
                     )
                 nc.scalar.activation(out=act[:, cols], in_=bank[:], func=GELU, bias=bias[:, m : m + 1])
-            nc.vector.tensor_tensor(result[:, m, :], gates[m][:].indirect(offsets[:]), act[:], MULT)
+            last = m == M_TILES - 1
+            width = N_TILE if m == 0 or last else S
+            for j0 in range(0, S, width):
+                cols = slice(j0, j0 + width)
+                picks = offsets[:, j0 // 16 : (j0 + width) // 16]
+                nc.vector.tensor_tensor(result[:, m, cols], gates[m][:].indirect(picks), act[:, cols], MULT)
+                if last:
+                    nc.sync.dma_start(out=out_rows[:, m, cols], in_=result[:, m, cols])
             if m + 1 in STORE_ENDS:
                 queue = nc.scalar if m < EARLY_STORES else nc.sync
                 queue.dma_start(out=out_rows[:, stored : m + 1, :], in_=result[:, stored : m + 1, :])

@@ -74,11 +74,11 @@ def tile_list_tabgate_gelu_kernel(tc, tab_words, tab_scales, w, gT, b, offs, out
 
         nc.vector.tensor_copy(picked_scales[:], scale_table[:].bitcast(U8).indirect(offsets[:]))
         for r in range(4):
-            for q in (0, 2, 1, 3):
-                first = 4 * (4 * q + r)
+            for a in range(PASSES):
+                row = 4 * r + a
                 nc.gpsimd.dma_start(
-                    out=v_scales[32 * q + r : 32 * q + 4 * PASSES : 4, :],
-                    in_=picked_scales[first : first + PASSES, :].bitcast(I32),
+                    out=v_scales[4 * a + r : P : 32, :],
+                    in_=picked_scales[row : 64 : 16, :].bitcast(I32),
                 )
 
         for a in range(PASSES):

@@ -50,8 +50,7 @@ def tile_list_tabgate_gelu_kernel(tc, tab_words, tab_scales, w, gT, b, offs, out
         scale_words = tab_scales.bitcast(I32)
         nc.sync.dma_start(offsets[:], offs)
         for a in range(PASSES):
-            for i0 in (0, 8):
-                nc.gpsimd.dma_start(out=scale_table[4 * i0 + a : 4 * i0 + 32 : 4, :], in_=scale_words[a, i0 : i0 + 8])
+            nc.gpsimd.dma_start(out=scale_table[32 + a : 96 : 4, :], in_=scale_words[a])
         nc.vector.memset(v_scales[:], 0)
 
         w_raw = []
@@ -75,10 +74,10 @@ def tile_list_tabgate_gelu_kernel(tc, tab_words, tab_scales, w, gT, b, offs, out
         nc.vector.tensor_copy(picked_scales[:], scale_table[:].bitcast(U8).indirect(offsets[:]))
         for r in range(4):
             for a in range(PASSES):
-                row = 4 * r + a
+                row = 32 + 4 * r + a
                 nc.gpsimd.dma_start(
                     out=v_scales[4 * a + r : P : 32, :],
-                    in_=picked_scales[row : 64 : 16, :].bitcast(I32),
+                    in_=picked_scales[row : 96 : 16, :].bitcast(I32),
                 )
 
         for a in range(PASSES):
@@ -127,7 +126,14 @@ def tile_list_tabgate_gelu_kernel(tc, tab_words, tab_scales, w, gT, b, offs, out
                 nc.vector.tensor_tensor(result[:, m, cols], gates[m][:].indirect(picks), act[:, cols], MULT)
                 if last:
                     nc.sync.dma_start(out=out_rows[:, m, cols], in_=result[:, m, cols])
-            if m + 1 in STORE_ENDS:
+            if m == 0:
+                nc.scalar.dma_start(out=out_rows[32:96, m, :], in_=result[32:96, m, :])
+                for first in (0, 96):
+                    for r in range(4):
+                        part = slice(first + r, first + 32, 4)
+                        nc.gpsimd.dma_start(out=out_rows[part, m, :], in_=result[part, m, :])
+                stored = 1
+            elif m + 1 in STORE_ENDS:
                 queue = nc.scalar if m < EARLY_STORES else nc.sync
                 queue.dma_start(out=out_rows[:, stored : m + 1, :], in_=result[:, stored : m + 1, :])
                 stored = m + 1

@@ -56,7 +56,8 @@ def tile_list_tabgate_gelu_kernel(tc, tab_words, tab_scales, w, gT, b, offs, out
         w_raw = []
         for a in range(PASSES):
             raw = stream.tile([P, PACK, M], F32, name="stream")
-            nc.sync.dma_start(out=raw[:], in_=w[a * K_PASS : (a + 1) * K_PASS, :].rearrange("(p j) n -> p j n", j=PACK))
+            queue = nc.scalar if a == 0 else nc.sync
+            queue.dma_start(out=raw[:], in_=w[a * K_PASS : (a + 1) * K_PASS, :].rearrange("(p j) n -> p j n", j=PACK))
             w_raw.append(raw)
             if a == 0:
                 nc.sync.dma_start(out=bias[:], in_=b.rearrange("(p m) -> p m", m=M_TILES))

@@ -25,6 +25,7 @@ QUANT_TILES = 4
 STREAM_BUFS = 7
 STORE_ENDS = (1, 2, 3, 6, 7)
 EARLY_STORES = 3
+UNEVEN_ROWS = (12, 108, 8)
 
 
 def tile_list_tabgate_gelu_kernel(tc, tab_words, tab_scales, w, gT, b, offs, out):
@@ -79,6 +80,7 @@ def tile_list_tabgate_gelu_kernel(tc, tab_words, tab_scales, w, gT, b, offs, out
                 nc.gpsimd.dma_start(
                     out=v_scales[4 * a + r : P : 32, :],
                     in_=picked_scales[row : 96 : 16, :].bitcast(I32),
+                    max_dma_last_dim=S // 2,
                 )
 
         for a in range(PASSES):
@@ -128,11 +130,11 @@ def tile_list_tabgate_gelu_kernel(tc, tab_words, tab_scales, w, gT, b, offs, out
                 if last:
                     nc.sync.dma_start(out=out_rows[:, m, cols], in_=result[:, m, cols])
             if m == 0:
-                nc.scalar.dma_start(out=out_rows[32:96, m, :], in_=result[32:96, m, :])
-                for first in (0, 96):
-                    for r in range(4):
-                        part = slice(first + r, first + 32, 4)
-                        nc.gpsimd.dma_start(out=out_rows[part, m, :], in_=result[part, m, :])
+                first = 0
+                for count in UNEVEN_ROWS:
+                    part = slice(first, first + count)
+                    nc.gpsimd.dma_start(out=out_rows[part, m, :], in_=result[part, m, :], max_dma_last_dim=2 * S)
+                    first += count
                 stored = 1
             elif m + 1 in STORE_ENDS:
                 queue = nc.scalar if m < EARLY_STORES else nc.sync

@@ -25,7 +25,8 @@ QUANT_TILES = 4
 STREAM_BUFS = 7
 STORE_ENDS = (1, 2, 3, 6, 7)
 EARLY_STORES = 3
-UNEVEN_ROWS = (12, 108, 8)
+UNEVEN_COLS = 1280
+UNEVEN_ROWS = ((14, UNEVEN_COLS // 2), (100, UNEVEN_COLS // 2), (8, UNEVEN_COLS // 2), (6, UNEVEN_COLS))
 
 
 def tile_list_tabgate_gelu_kernel(tc, tab_words, tab_scales, w, gT, b, offs, out):
@@ -103,6 +104,8 @@ def tile_list_tabgate_gelu_kernel(tc, tab_words, tab_scales, w, gT, b, offs, out
                 nc.vector.tensor_copy(v_codes[a][:, j0 : j0 + width], tables[a][:].bitcast(U32).indirect(picks))
 
         out_rows = out.rearrange("(p m) j -> p m j", m=M_TILES)
+        out_flat = out.rearrange("(p m) j -> p (m j)", m=M_TILES)
+        result_flat = result[:].rearrange("p m j -> p (m j)")
         stored = 0
         for m in range(M_TILES):
             rows = slice(m * P, (m + 1) * P)
@@ -131,12 +134,12 @@ def tile_list_tabgate_gelu_kernel(tc, tab_words, tab_scales, w, gT, b, offs, out
                     nc.sync.dma_start(out=out_rows[:, m, cols], in_=result[:, m, cols])
             if m == 0:
                 first = 0
-                for count in UNEVEN_ROWS:
+                for count, piece in UNEVEN_ROWS:
                     part = slice(first, first + count)
-                    nc.gpsimd.dma_start(out=out_rows[part, m, :], in_=result[part, m, :], max_dma_last_dim=2 * S)
+                    nc.gpsimd.dma_start(out=out_flat[part, :UNEVEN_COLS], in_=result_flat[part, :UNEVEN_COLS], max_dma_last_dim=4 * piece)
                     first += count
-                stored = 1
+                stored = UNEVEN_COLS
             elif m + 1 in STORE_ENDS:
                 queue = nc.scalar if m < EARLY_STORES else nc.sync
-                queue.dma_start(out=out_rows[:, stored : m + 1, :], in_=result[:, stored : m + 1, :])
-                stored = m + 1
+                queue.dma_start(out=out_flat[:, stored : (m + 1) * S], in_=result_flat[:, stored : (m + 1) * S])
+                stored = (m + 1) * S

@@ -23,8 +23,8 @@ N_TILE = 512
 M_TILES = M // P
 QUANT_TILES = 4
 STREAM_BUFS = 7
-STORE_ENDS = (1, 2, 3, 6, 7)
-EARLY_STORES = 3
+STORE_ENDS = (3, 4, 5, 6, 7)
+BESIDE_LOADS = (3, 4)
 UNEVEN_COLS = 1280
 UNEVEN_ROWS = ((14, UNEVEN_COLS // 2), (100, UNEVEN_COLS // 2), (8, UNEVEN_COLS // 2), (6, UNEVEN_COLS))
 
@@ -140,6 +140,6 @@ def tile_list_tabgate_gelu_kernel(tc, tab_words, tab_scales, w, gT, b, offs, out
                     first += count
                 stored = UNEVEN_COLS
             elif m + 1 in STORE_ENDS:
-                queue = nc.scalar if m < EARLY_STORES else nc.sync
+                queue = nc.scalar if m in BESIDE_LOADS else nc.sync
                 queue.dma_start(out=out_flat[:, stored : (m + 1) * S], in_=result_flat[:, stored : (m + 1) * S])
                 stored = (m + 1) * S

from contextlib import ExitStack

import concourse.mybir as mybir

K, M, T, S = 1536, 1024, 4096, 1536
FLOPS = 2 * K * M * S

F32 = mybir.dt.float32
BF16 = mybir.dt.bfloat16
I32 = mybir.dt.int32
U32 = mybir.dt.uint32
U16 = mybir.dt.uint16
U8 = mybir.dt.uint8
FP8X4 = mybir.dt.float8_e4m3fn_x4
GELU = mybir.ActivationFunctionType.Gelu_apprx_tanh
MULT = mybir.AluOpType.mult

P = 128
PACK = 4
K_PASS = P * PACK
PASSES = K // K_PASS
N_TILE = 512
M_TILES = M // P
QUANT_TILES = 4
STREAM_BUFS = 7
STORE_ENDS = (3, 4, 5, 6, 7)
BESIDE_LOADS = (3, 4)
UNEVEN_COLS = 1280
UNEVEN_ROWS = ((14, UNEVEN_COLS // 2), (100, UNEVEN_COLS // 2), (8, UNEVEN_COLS // 2), (6, UNEVEN_COLS))


def tile_list_tabgate_gelu_kernel(tc, tab_words, tab_scales, w, gT, b, offs, out):
    nc = tc.nc
    with ExitStack() as ctx:
        keep = ctx.enter_context(tc.tile_pool(name="keep", bufs=1))
        stream = ctx.enter_context(tc.tile_pool(name="stream", bufs=STREAM_BUFS))
        stage = ctx.enter_context(tc.tile_pool(name="stage", bufs=3))
        acts = ctx.enter_context(tc.tile_pool(name="acts", bufs=3))
        psum = ctx.enter_context(tc.psum_pool(name="psum", bufs=8))

        offsets = keep.tile([P, S // 16], U16, name="offsets")
        scale_table = keep.tile([P, T // 4], I32, name="scale_table", align_bytes=64)
        bias = keep.tile([P, M_TILES], F32, name="bias")
        w_codes = keep.tile([P, PASSES, M], U32, name="w_codes", align_bytes=64)
        w_scales = keep.tile([P, PASSES, M], U8, name="w_scales", align_bytes=64)
        picked_scales = keep.tile([P, S], U8, name="picked_scales", align_bytes=64)
        v_scales = keep.tile([P, S // 4], I32, name="v_scales", align_bytes=64)
        v_codes = [keep.tile([P, S], U32, name=f"v_codes{a}", align_bytes=64) for a in range(PASSES)]
        result = keep.tile([P, M_TILES, S], F32, name="result")

        nc.vector.memset(scale_table[:], 0)
        scale_words = tab_scales.bitcast(I32)
        nc.sync.dma_start(offsets[:], offs)
        for a in range(PASSES):
            nc.gpsimd.dma_start(out=scale_table[32 + a : 96 : 4, :], in_=scale_words[a])
        nc.vector.memset(v_scales[:], 0)

        w_raw = []
        for a in range(PASSES):
            raw = stream.tile([P, PACK, M], F32, name="stream")
            queue = nc.scalar if a == 0 else nc.sync
            queue.dma_start(out=raw[:], in_=w[a * K_PASS : (a + 1) * K_PASS, :].rearrange("(p j) n -> p j n", j=PACK))
            w_raw.append(raw)
            if a == 0:
                nc.sync.dma_start(out=bias[:], in_=b.rearrange("(p m) -> p m", m=M_TILES))
        tables = []
        for a in range(PASSES):
            table = stream.tile([P, T], I32, name="stream")
            nc.sync.dma_start(out=table[:], in_=tab_words[a].rearrange("p t i -> p (t i)").bitcast(I32))
            tables.append(table)
        gates = []
        for m in range(M_TILES):
            gate = stream.tile([P, T], F32, name="stream")
            nc.sync.dma_start(out=gate[:], in_=gT.rearrange("(p m) t -> m p t", m=M_TILES)[m])
            gates.append(gate)

        nc.vector.tensor_copy(picked_scales[:], scale_table[:].bitcast(U8).indirect(offsets[:]))
        for r in range(4):
            for a in range(PASSES):
                row = 32 + 4 * r + a
                nc.gpsimd.dma_start(
                    out=v_scales[4 * a + r : P : 32, :],
                    in_=picked_scales[row : 96 : 16, :].bitcast(I32),
                    max_dma_last_dim=S // 2,
                )

        for a in range(PASSES):
            for m0 in range(0, M_TILES, QUANT_TILES):
                cols = slice(m0 * P, (m0 + QUANT_TILES) * P)
                grouped = stage.tile([P, QUANT_TILES, P, PACK], BF16, name="grouped", align_bytes=64)
                source = w_raw[a][:].rearrange("p j (q m) -> p q m j", m=M_TILES)[:, :, m0 : m0 + QUANT_TILES, :]
                target = grouped[:].rearrange("p m q j -> p q m j")
                nc.scalar.copy(out=target, in_=source)
                nc.vector.quantize_mx(
                    out=w_codes[:, a, cols].bitcast(FP8X4),
                    scales=w_scales[:, a, cols],
                    in_=grouped[:].rearrange("p m q j -> p (m q j)"),
                )

        for a in range(PASSES):
            width = N_TILE if a == PASSES - 1 else S
            for j0 in range(0, S, width):
                picks = offsets[:, j0 // 16 : (j0 + width) // 16]
                nc.vector.tensor_copy(v_codes[a][:, j0 : j0 + width], tables[a][:].bitcast(U32).indirect(picks))

        out_rows = out.rearrange("(p m) j -> p m j", m=M_TILES)
        out_flat = out.rearrange("(p m) j -> p (m j)", m=M_TILES)
        result_flat = result[:].rearrange("p m j -> p (m j)")
        stored = 0
        for m in range(M_TILES):
            rows = slice(m * P, (m + 1) * P)
            act = acts.tile([P, S], F32, name="act")
            for j0 in range(0, S, N_TILE):
                cols = slice(j0, j0 + N_TILE)
                bank = psum.tile([P, N_TILE], F32, name="bank")
                for a in range(PASSES):
                    nc.tensor.matmul_mx(
                        out=bank[:],
                        lhsT=w_codes[:, a, rows].bitcast(FP8X4),
                        lhsT_scale=w_scales[:, a, rows],
                        rhs=v_codes[a][:, cols].bitcast(FP8X4),
                        rhs_scale=v_scales[4 * a : P, :].bitcast(U8)[:, cols],
                        start=(a == 0),
                        stop=(a == PASSES - 1),
                    )
                nc.scalar.activation(out=act[:, cols], in_=bank[:], func=GELU, bias=bias[:, m : m + 1])
            last = m == M_TILES - 1
            width = N_TILE if m == 0 or last else S
            for j0 in range(0, S, width):
                cols = slice(j0, j0 + width)
                picks = offsets[:, j0 // 16 : (j0 + width) // 16]
                nc.vector.tensor_tensor(result[:, m, cols], gates[m][:].indirect(picks), act[:, cols], MULT)
                if last:
                    nc.sync.dma_start(out=out_rows[:, m, cols], in_=result[:, m, cols])
            if m == 0:
                first = 0
                for count, piece in UNEVEN_ROWS:
                    part = slice(first, first + count)
                    nc.gpsimd.dma_start(out=out_flat[part, :UNEVEN_COLS], in_=result_flat[part, :UNEVEN_COLS], max_dma_last_dim=4 * piece)
                    first += count
                stored = UNEVEN_COLS
            elif m + 1 in STORE_ENDS:
                queue = nc.scalar if m in BESIDE_LOADS else nc.sync
                queue.dma_start(out=out_flat[:, stored : (m + 1) * S], in_=result_flat[:, stored : (m + 1) * S])
                stored = (m + 1) * S
